import numpy as np, ml_dtypes
CORES = [36,164,52,180,100,228,116,244]
N = 8
import mx_ref
BF = ml_dtypes.bfloat16
def entries(a):
    return np.ascontiguousarray(a.T).reshape(-1)
def table(e):
    return np.ascontiguousarray(np.reshape(e, (-1, 16)).T).astype(np.int32)
def cols(t, e):
    v = np.concatenate([t.reshape(128, -1, 4), np.zeros((128, 1, 4), BF)], axis=1)
    return np.ascontiguousarray(v[:, e]).reshape(128, -1)
def f(rng, *shape):
    return mx_ref.flush((rng.standard_normal(shape, dtype=np.float32) * np.exp2(rng.integers(-2, 3, shape[:-1] + (1,)))).astype(BF))
def wide(rng, *shape, cols=0):
    v = rng.standard_normal(shape, dtype=np.float32) * np.exp2(rng.integers(-12, 13, shape)).astype(np.float32)
    if cols: v *= np.repeat(np.exp2(rng.integers(-cols, cols + 1, shape[:-2] + (1, shape[-1] // 4))) * (rng.random(shape[:-2] + (1, shape[-1] // 4)) > 0.0625), 4, axis=-1).astype(np.float32)
    return mx_ref.flush(v.astype(BF))
T, CAPP = 256, 48
def lists(rng, full=False, skew=False, single=False, back=False):
    if full:
        v = rng.permutation(([CAPP] * (T // CAPP) + [T % CAPP] + [0] * N)[:N])
        n = v[(np.arange(N)[None, :] - np.arange(N)[:, None]) % N][rng.permutation(N)][:, rng.permutation(N)]
    else:
        n = np.full((N, N), T // N)
        for _ in range(20 * N):
            (s, t), (d, e) = rng.permutation(N)[:2], rng.permutation(N)[:2]
            k = rng.integers(0, min(n[s, d], n[t, e], CAPP - n[s, e], CAPP - n[t, d]) + 1)
            n[s, d] -= k; n[t, e] -= k; n[s, e] += k; n[t, d] += k
    a = np.full((N, N * CAPP), -1)
    for s in range(N):
        parts = np.split(rng.permutation(T), np.cumsum(n[s])[:-1])
        for d in range(N): a[s, d * CAPP + rng.permutation(CAPP)[:n[s, d]]] = parts[d]
    p, u, o = [], [], []
    for r in range(N):
        used = np.flatnonzero(a[:, r * CAPP:(r + 1) * CAPP].reshape(-1) >= 0)
        p.append(table(used[::-1] if back else rng.permutation(used)))
        h = rng.integers(0, N)
        c = rng.integers(0, 2, N) if full else (np.full(N, -1) if rng.random() < 0.5 else rng.integers(0, 2, N)) if single else rng.integers(-1, 2, N)
        if c[h] < 0: c[h] = rng.integers(0, 2)
        named = np.flatnonzero(c >= 0)
        if single: named = np.array([h])
        if skew:
            m = rng.integers(T // 2 + 1, T + 1)
            e = np.sort(np.concatenate([np.full(m, h), rng.choice(named, T - m)]))
        elif full: e = np.sort(np.concatenate([named, rng.choice(named, T - N)]))
        else: e = np.repeat(named, np.diff(np.concatenate([[0], np.sort(rng.integers(0, T + 1, len(named) - 1)), [T]])))
        u.append(table(np.concatenate([c, np.full(16 - N, -1)]))); o.append(table(e))
    return {"send": np.stack([table(k) for k in a]), "place": np.stack(p), "sel": np.stack(u), "of": np.stack(o)}
def setup_inputs(rng):
    return {"x": f(rng, N, 128, 4 * T), "w": f(rng, N, 256, 512), **lists(rng)}
def setup_inputs_full(rng):
    return {**setup_inputs(rng), **lists(rng, full=True)}
def setup_inputs_reversed(rng):
    return {**setup_inputs(rng), **lists(rng, back=True)}
def setup_inputs_single(rng):
    return {**setup_inputs(rng), **lists(rng, single=True)}
def setup_inputs_skew(rng):
    return {**setup_inputs(rng), **lists(rng, skew=True)}
def setup_inputs_spread(rng):
    d = setup_inputs(rng); d["x"] = wide(rng, N, 128, 4 * T, cols=8); return d
def check_inputs(d):
    b = []
    for k in ("x", "w"):
        a = np.abs(d[k].astype(np.float32))
        if not ((a == 0) | ((a >= 2.0 ** -30) & (a <= 2.0 ** 30))).all(): b.append(k)
    sends = np.stack([entries(d["send"][r]) for r in range(N)])
    for r in range(N):
        c, p, u, e = sends[r], entries(d["place"][r]), entries(d["sel"][r]), entries(d["of"][r])
        if c.min() < -1 or not np.array_equal(np.sort(c[c >= 0]), np.arange(T)): b.append("send")
        if not np.array_equal(np.sort(p), np.flatnonzero(sends[:, r * CAPP:(r + 1) * CAPP].reshape(-1) >= 0)): b.append("place")
        if u.min() < -1 or u.max() > 1 or (u[N:] != -1).any(): b.append("sel")
        if e.min() < 0 or e.max() >= N or (np.diff(e) < 0).any() or (u[e] < 0).any(): b.append("of")
    return b
def reference(x, w, send, place, sel, of):
    W = [[mx_ref.quantize(w[h][128 * m:128 * m + 128]) for m in range(2)] for h in range(N)]
    y = np.zeros((N, 128, T), np.float32)
    for r in range(N):
        slots = np.concatenate([cols(x[s], entries(send[s])[r * CAPP:(r + 1) * CAPP]) for s in range(N)], axis=1)
        X = mx_ref.quantize(cols(slots, entries(place[r])))
        u, e = entries(sel[r]), entries(of[r])
        for h in range(N):
            i = e == h
            if i.any(): y[r][:, i] = mx_ref.matmul(W[h][u[h]], X)[:, i]
    return {"y": y}

from concourse.bass import DstId, RemoteDMATransfer
from concourse.mybir import dt, AluOpType, ActivationFunctionType

N, CAPP, TC = 8, 48, 256
SLOTS = N * CAPP
BOTH = (1,)
PATH_E = {1: "D", 2: "D", 3: 1, 4: 2, 5: "D", 6: "D", 7: "D"}
PATH_X = {1: 1, 2: 1, 3: 2, 4: 2, 5: 3, 6: "D", 7: "D"}
GROUPS = ((2, 3), (4, 5), (6, 7))
ORDER = (0, 1, 2, 5, 3, 6, 7, 4)
VPART = 26
NH = 3
NE = N + len(BOTH)
HALF = SLOTS // 2

F8 = "float8_e4m3fn_x4"
SCRATCH = {
    "ldr": ("dram", [128, 1], "int32"), "lland": ("dram", [N, 128, 1], "int32"),
    "snd": ("sbuf", [128, 24], "int32"), "off4": ("sbuf", [128, 24], "uint16"),
    "pl": ("sbuf", [128, 16], "int32"), "ofl": ("sbuf", [128, 16], "int32"),
    "selrow": ("sbuf", [1, 16], "int32"), "sf": ("sbuf", [1, 16], "float32"), "selb": ("sbuf", [128, 16], "float32"),
    "lrow": ("sbuf", [1, 16], "int32"), "lf": ("sbuf", [1, 16], "float32"), "lb": ("sbuf", [128, 16], "float32"),
    "ip": ("sbuf", [128, 32], "int32"), "iq": ("sbuf", [128, 32], "int32"), "ip15": ("sbuf", [128, 32], "int32"),
    "ib": ("sbuf", [128, 32], "int32"), "offo": ("sbuf", [128, 32], "uint16"),
    "offe": ("sbuf", [128, 64 * len(GROUPS)], "uint16"),
    "ac0": ("sbuf", [128, 16], "float32"), "offy": ("sbuf", [128, 16], "uint16"), "sel3": ("sbuf", [128, 16], "float32"),
    "xs": ("sbuf", [128, 4 * TC], "bfloat16"), "ws": ("sbuf", [128, 1024], "bfloat16"),
    "xt": ("sbuf", [128, 4 * SLOTS], "bfloat16"), "eo": ("sbuf", [128, 512], "bfloat16"),
    "xq": ("sbuf", [128, SLOTS], F8), "xqs": ("sbuf", [128, SLOTS], "uint8"),
    "wq": ("sbuf", [128, 256], F8), "wqs": ("sbuf", [128, 256], "uint8"),
    "xl": ("sbuf", [128, SLOTS], F8), "xls": ("sbuf", [128, SLOTS], "uint8"),
    "el": ("sbuf", [128, 128 * NE], F8), "els": ("sbuf", [128, 128 * NE], "uint8"),
    "ps": ("psum", [128, 4096], "float32"), "res": ("sbuf", [128, SLOTS * NE], "float32"), "yb": ("sbuf", [128, TC], "float32"),
    "hx": ("sbuf", [128, 2 * CAPP], F8), "hxs": ("sbuf", [128, 2 * CAPP], "uint8"),
    "he": ("sbuf", [128, 128], F8), "hes": ("sbuf", [128, 128], "uint8"),
}
for _i in range(len(BOTH)):
    SCRATCH["ta%d" % _i] = ("sbuf", [128, 16], "float32")
    SCRATCH["tb%d" % _i] = ("sbuf", [128, 16], "float32")
    SCRATCH["aa%d" % _i] = ("sbuf", [128, 16], "float32")
    SCRATCH["ab%d" % _i] = ("sbuf", [128, 16], "float32")
SCRATCH["ac1"] = ("sbuf", [128, 16], "float32")
for _i in range(len(GROUPS)):
    SCRATCH["eg%d" % _i] = ("sbuf", [128, 512 * len(GROUPS[_i])], "bfloat16")
    SCRATCH["gq%d" % _i] = ("sbuf", [128, 128 * len(GROUPS[_i])], F8)
    SCRATCH["gs%d" % _i] = ("sbuf", [128, 128 * len(GROUPS[_i])], "uint8")

SEMAPHORES = ["loc", "li", "xin", "hxc", "hxs", "hec", "hes", "ldr", "lown", "lsel", "lw", "lsnd", "lx", "lpl", "lrow", "xo", "y0", "y1",
              "iot", "ib0", "ib", "sf", "selb", "offo", "qw", "off4", "xgv", "xgs", "qx", "og", "qo", "lf", "lb", "s3", "yv", "ys", "offy",
              "evv", "evs"]
SEMAPHORES += ["e%d" % k for k in range(1, N)] + ["ac%d" % k for k in range(2 + 4 * len(BOTH))]
SEMAPHORES += ["%s%d" % (a, k) for a in ("go", "gv", "gs", "gq") for k in range(len(GROUPS))]
SEMAPHORES += ["mm%d_%d" % (k, h) for k in range(NE) for h in range(2)] + ["ev%d_%d" % (k, h) for k in range(NE - 4) for h in range(2)]


def share(engs, n):
    w = 1
    while 2 * w * n <= len(engs):
        w *= 2
    return [engs[i * w:(i + 1) * w] for i in range(n)]


def bits(engs):
    m = 0
    for e in engs:
        m |= 1 << e
    return m


def helpers_of(c, topo):
    return [k for k in topo.cores_of(c) if topo.die(k) != topo.die(c)][:NH]


def bases(r):
    out, n = [], 0
    for h in range(N):
        out.append(n)
        n += 2 if (r - h) % N in BOTH else 1
    return out


def u8(ap):
    return ap.bitcast(dt.uint8)


def rank_program(g, core, T, topo):
    S = T.sem
    rank = T.rank_of(core)
    sent = [0]

    def call(items):
        tr = []
        for cores, engs, src, dsts, sem in items:
            ids = []
            for c in cores:
                rid, pid = topo.addr(c, core)
                ids.append(DstId(rid=rid, pnc=pid))
            tr.append(RemoteDMATransfer(dst_ids=ids, dma_engine_mask=bits(engs), remote_sem=sem, srcs=[src], dsts=dsts))
            sent[0] += len(engs)
        g.remote_dma_fused(tr, local_sem=S.loc)

    if rank is None:
        own = [c for c in topo.cores_of(core) if T.rank_of(c) is not None]
        if not own or core not in helpers_of(own[0], topo):
            return
        r = T.rank_of(own[0])
        me = helpers_of(own[0], topo).index(core) + 1
        dest = lambda k: T.cores[(r + k) % N]
        off = topo.engines(core, dest(1))
        hi = [e for e in topo.engines(own[0], core) if e not in topo.engines(own[0], dest(1))]
        xk = [k for k in range(1, N) if PATH_X[k] == me]
        ek = [k for k in range(1, N) if PATH_E[k] == me]
        if xk:
            same = [h for h in range(1, NH + 1) if sum(PATH_X[k] == h for k in range(1, N)) == len(xk)]
            n = len(share(hi, len(same))[0])
            parts = share(off, len(xk))
            g.wait_ge(S.hxc, n)
            call([([dest(k)], parts[i], u8(T.hx[:, CAPP * i:CAPP * (i + 1)]), [u8(T.xl[:, CAPP * r:CAPP * (r + 1)])], S.xin) for i, k in enumerate(xk)])
            g.wait_ge(S.hxs, n)
            call([([dest(k)], parts[i], T.hxs[:, CAPP * i:CAPP * (i + 1)], [T.xls[:, CAPP * r:CAPP * (r + 1)]], S.xin) for i, k in enumerate(xk)])
        for k in ek:
            b = 128 * bases((r + k) % N)[r]
            g.wait_ge(S.hec, len(hi))
            call([([dest(k)], off, u8(T.he[:]), [u8(T.el[:, b:b + 128])], S["e%d" % k])])
            g.wait_ge(S.hes, len(hi))
            call([([dest(k)], off, T.hes[:], [T.els[:, b:b + 128]], S["e%d" % k])])
        if sent[0]:
            g.wait_ge(S.loc, sent[0])
        return

    r = rank
    dest = lambda k: T.cores[(r + k) % N]
    hlp = helpers_of(core, topo)
    lo = topo.engines(core, dest(1))
    hi = [e for e in topo.engines(core, hlp[0]) if e not in lo]
    base = bases(r)
    V, C, SY, TE = g.vector, g.scalar, g.sync, g.tensor
    COPY = ActivationFunctionType.Copy
    OP = AluOpType

    SY.dma_start(T.ldr[0:16, :], T.sel[:, :]).then_inc(S.ldr, 16)
    SY.dma_start(T.ldr[16:128, :], T.place[0:7, :]).then_inc(S.ldr, 16)
    SY.dma_start(T.xs[:], T.x[:]).then_inc(S.lx, 16)
    C.dma_start(T.ws[:, 0:512], T.w[0:128, :]).then_inc(S.lw, 16)
    C.dma_start(T.ws[:, 512:1024], T.w[128:256, :]).then_inc(S.lw, 16)
    for q in range(8):
        (SY if q < 4 else C).dma_start(T.snd[16 * q:16 * q + 16, :], T.send[:, :]).then_inc(S.lsnd, 16)
    SY.dma_start(T.selrow[0:1, :], T.sel[:, :]).then_inc(S.lsel, 16)
    SY.dma_start(T.lland[r, 0:16, :], T.sel[:, :]).then_inc(S.lown, 16)

    g.iota(T.ip[:], [[0, 32]], 0, 1).then_inc(S.iot, 1)
    g.iota(T.iq[:], [[16, 32]], 0, 0).then_inc(S.iot, 1)
    V.wait_ge(S.iot, 2)
    V.tensor_scalar(T.ip15[:], T.ip[:], 15, None, OP.bitwise_and).then_inc(S.ib0, 1)
    V.wait_ge(S.ib0, 1)
    V.tensor_tensor(T.ib[:], T.ip15[:], T.iq[:], OP.add).then_inc(S.ib, 1)

    g.wait_ge(S.ldr, 32)
    call([([dest(k) for k in range(1, N)], lo[:1], T.ldr[:, :], [T.lland[r] for k in range(1, N)], S.li)])

    V.wait_ge(S.lsel, 16)
    V.tensor_scalar(T.sf[0:1, :], T.selrow[0:1, :], 0.0, 512.0, OP.max, OP.mult).then_inc(S.sf, 1)
    g.wait_ge(S.sf, 1)
    g.partition_broadcast(T.selb[:], T.sf[0:1, :], 128).then_inc(S.selb, 1)
    V.wait_ge(S.lsnd, 128)
    n = 1
    V.tensor_scalar(T.off4[:, 0:3 * (N - r)], T.snd[:, 3 * r:24], 0.0, 4.0, OP.max, OP.mult).then_inc(S.off4, 1)
    if r:
        V.tensor_scalar(T.off4[:, 3 * (N - r):24], T.snd[:, 0:3 * r], 0.0, 4.0, OP.max, OP.mult).then_inc(S.off4, 1)
        n = 2
    V.wait_ge(S.lw, 32)
    V.quantize_mx(T.wq[:], T.wqs[:], T.ws[:]).then_inc(S.qw, 1)

    V.wait_ge(S.off4, n)
    V.wait_ge(S.lx, 16)
    for t in (0, 1):
        V.tensor_copy(T.xt[:, t:4 * SLOTS:4], T.xs[:, t:4 * TC].indirect(T.off4[:, 0:24])).then_inc(S.xgv, 1)
    C.wait_ge(S.off4, n)
    C.wait_ge(S.lx, 16)
    for t in (2, 3):
        C.activation(T.xt[:, t:4 * SLOTS:4], T.xs[:, t:4 * TC].indirect(T.off4[:, 0:24]), COPY).then_inc(S.xgs, 1)
    V.wait_ge(S.selb, 1)
    V.wait_ge(S.ib, 1)
    V.tensor_scalar(T.offo[:], T.ib[:], T.selb[:, r:r + 1], None, OP.add).then_inc(S.offo, 1)
    V.wait_ge(S.xgv, 2)
    V.wait_ge(S.xgs, 2)
    V.quantize_mx(T.xq[:], T.xqs[:], T.xt[:]).then_inc(S.qx, 1)
    C.wait_ge(S.offo, 1)
    C.wait_ge(S.lw, 32)
    C.activation(T.eo[:], T.ws[:].indirect(T.offo[:]), COPY).then_inc(S.og, 1)
    V.wait_ge(S.og, 1)
    b = 128 * base[r]
    V.quantize_mx(T.el[:, b:b + 128], T.els[:, b:b + 128], T.eo[:]).then_inc(S.qo, 1)

    g.wait_ge(S.qw, 1)
    parts = share(lo, len(BOTH))
    for sc in (0, 1):
        it = []
        for i, k in enumerate(BOTH):
            b = 128 * bases((r + k) % N)[r]
            src = T.wqs[:] if sc else u8(T.wq[:])
            dst = T.els[:, b:b + 256] if sc else u8(T.el[:, b:b + 256])
            it.append(([dest(k)], parts[i], src, [dst], S["e%d" % k]))
        call(it)

    sets = {}
    for h in range(1, NH + 1):
        ks = [k for k in range(1, N) if PATH_X[k] == h]
        if ks:
            sets.setdefault(len(ks), []).append((h, ks))
    xd = [k for k in range(1, N) if PATH_X[k] == "D"]
    if xd:
        sets.setdefault(1, [])
    g.wait_ge(S.qx, 1)
    for sc in (0, 1):
        for w in sorted(sets, reverse=True):
            it = []
            for i, (h, ks) in enumerate(sets[w]):
                a = CAPP * ks[0]
                src = T.xqs[:, a:a + CAPP * w] if sc else u8(T.xq[:, a:a + CAPP * w])
                dst = T.hxs[:, 0:CAPP * w] if sc else u8(T.hx[:, 0:CAPP * w])
                it.append(([hlp[h - 1]], share(hi, len(sets[w]))[i], src, [dst], S.hxs if sc else S.hxc))
            if w == 1:
                for i, k in enumerate(xd):
                    src = T.xqs[:, CAPP * k:CAPP * (k + 1)] if sc else u8(T.xq[:, CAPP * k:CAPP * (k + 1)])
                    dst = T.xls[:, CAPP * r:CAPP * (r + 1)] if sc else u8(T.xl[:, CAPP * r:CAPP * (r + 1)])
                    it.append(([dest(k)], share(lo, len(xd))[i], src, [dst], S.xin))
            call(it)
    SY.wait_ge(S.qx, 1)
    SY.dma_start(u8(T.xl[:, CAPP * r:CAPP * (r + 1)]), u8(T.xq[:, 0:CAPP])).then_inc(S.xo, 16)
    SY.dma_start(T.xls[:, CAPP * r:CAPP * (r + 1)], T.xqs[:, 0:CAPP]).then_inc(S.xo, 16)

    SY.wait_ge(S.lown, 16)
    SY.wait_ge(S.li, N - 1)
    SY.dma_start(T.lrow[0:1, :], T.lland[:, r:r + 2, 0]).then_inc(S.lrow, 16)
    V.wait_ge(S.lrow, 16)
    V.tensor_scalar(T.lf[0:1, :], T.lrow[0:1, :], 0.0, 512.0, OP.max, OP.mult).then_inc(S.lf, 1)
    g.wait_ge(S.lf, 1)
    g.partition_broadcast(T.lb[:], T.lf[0:1, :], 128).then_inc(S.lb, 1)
    V.wait_ge(S.lb, 1)
    for q in range(8):
        SY.dma_start(T.pl[16 * q:16 * q + 16, :], T.place[:, :]).then_inc(S.lpl, 16)
        SY.dma_start(T.ofl[16 * q:16 * q + 16, :], T.of[:, :]).then_inc(S.lpl, 16)

    def offsets(j):
        for i, k in enumerate(GROUPS[j]):
            d = (r + k) % N
            V.tensor_scalar(T.offe[:, 64 * j + 32 * i:64 * j + 32 * i + 32], T.ib[:], T.lb[:, 2 * d:2 * d + 1], None, OP.add).then_inc(S["go%d" % j], 1)

    offsets(0)
    for j, ks in enumerate(GROUPS):
        eg, n = T["eg%d" % j], len(ks)
        vp = VPART * n // 2
        vp -= vp % 2
        V.wait_ge(S["go%d" % j], n)
        V.tensor_copy(eg[:, 0:16 * vp], T.ws[:].indirect(T.offe[:, 64 * j:64 * j + vp])).then_inc(S["gv%d" % j], 1)
        C.wait_ge(S["go%d" % j], n)
        C.activation(eg[:, 16 * vp:512 * n], T.ws[:].indirect(T.offe[:, 64 * j + vp:64 * j + 32 * n]), COPY).then_inc(S["gs%d" % j], 1)
        if j + 1 < len(GROUPS):
            offsets(j + 1)
        V.wait_ge(S["gv%d" % j], 1)
        V.wait_ge(S["gs%d" % j], 1)
        V.quantize_mx(T["gq%d" % j][:], T["gs%d" % j][:], eg[:]).then_inc(S["gq%d" % j], 1)
        g.wait_ge(S["gq%d" % j], 1)
        ds = [k for k in ks if PATH_E[k] == "D"]
        parts = share(lo, len(ds)) if ds else []
        for sc in (0, 1):
            it = []
            for i, k in enumerate(ks):
                src = T["gs%d" % j][:, 128 * i:128 * i + 128] if sc else u8(T["gq%d" % j][:, 128 * i:128 * i + 128])
                if PATH_E[k] == "D":
                    b = 128 * bases((r + k) % N)[r]
                    dst = T.els[:, b:b + 128] if sc else u8(T.el[:, b:b + 128])
                    it.append(([dest(k)], parts[ds.index(k)], src, [dst], S["e%d" % k]))
                else:
                    it.append(([hlp[PATH_E[k] - 1]], hi, src, [T.hes[:] if sc else u8(T.he[:])], S.hes if sc else S.hec))
            call(it)

    V.wait_ge(S.lpl, 256)
    V.tensor_scalar(T.ac0[:], T.ofl[:], float(SLOTS), None, OP.mult).then_inc(S.ac0, 1)
    V.tensor_scalar(T.sel3[:], T.selb[:], SLOTS / 512.0, None, OP.mult).then_inc(S.s3, 1)
    V.wait_ge(S.ac0, 1)
    V.tensor_tensor(T.ac1[:], T.ac0[:], T.pl[:], OP.add).then_inc(S.ac1, 1)
    V.wait_ge(S.s3, 1)
    acc, sn = T.ac1, 1
    for i, k in enumerate(BOTH):
        h = (r - k) % N
        V.tensor_scalar(T["ta%d" % i][:], T.ofl[:], float(h), float(SLOTS), OP.is_gt, OP.mult).then_inc(S["ac%d" % (4 * i + 2)], 1)
        V.tensor_scalar(T["tb%d" % i][:], T.ofl[:], float(h), T.sel3[:, h:h + 1], OP.is_equal, OP.mult).then_inc(S["ac%d" % (4 * i + 3)], 1)
        V.wait_ge(S["ac%d" % sn], 1)
        V.wait_ge(S["ac%d" % (4 * i + 2)], 1)
        V.tensor_tensor(T["aa%d" % i][:], acc[:], T["ta%d" % i][:], OP.add).then_inc(S["ac%d" % (4 * i + 4)], 1)
        V.wait_ge(S["ac%d" % (4 * i + 3)], 1)
        V.wait_ge(S["ac%d" % (4 * i + 4)], 1)
        V.tensor_tensor(T["ab%d" % i][:], T["aa%d" % i][:], T["tb%d" % i][:], OP.add).then_inc(S["ac%d" % (4 * i + 5)], 1)
        acc, sn = T["ab%d" % i], 4 * i + 5
    V.wait_ge(S["ac%d" % sn], 1)
    V.tensor_copy(T.offy[:], acc[:]).then_inc(S.offy, 1)

    def arrive_x(k):
        if PATH_X[k] == "D":
            return len(share(lo, len(xd))[0])
        return len(share(lo, sum(PATH_X[q] == PATH_X[k] for q in range(1, N)))[0])

    def arrive_e(k):
        if k in BOTH:
            return len(share(lo, len(BOTH))[0])
        if PATH_E[k] != "D":
            return len(lo)
        gr = [ks for ks in GROUPS if k in ks][0]
        return len(share(lo, sum(PATH_E[q] == "D" for q in gr))[0])

    TE.wait_ge(S.xo, 32)
    TE.wait_ge(S.xin, 2 * sum(arrive_x(k) for k in range(1, N)))
    prods = []
    for k in ORDER:
        b = base[(r - k) % N]
        prods.append((k, b, True))
        if k in BOTH:
            prods.append((k, b + 1, False))
    for i, (k, b, first) in enumerate(prods):
        if first:
            TE.wait_ge(S["e%d" % k] if k else S.qo, 2 * arrive_e(k) if k else 1)
        for h in (0, 1):
            bank = (2 * i + h) % 8
            if i >= 4:
                TE.wait_ge(S["ev%d_%d" % (i - 4, h)], 1)
            TE.matmul_mx(T.ps[:, 512 * bank:512 * bank + HALF], T.el[:, 128 * b:128 * b + 128], T.els[:, 128 * b:128 * b + 128],
                         T.xl[:, HALF * h:HALF * (h + 1)], T.xls[:, HALF * h:HALF * (h + 1)], True, True).then_inc(S["mm%d_%d" % (i, h)], 1)
            out = T.res[:, SLOTS * b + HALF * h:SLOTS * b + HALF * (h + 1)]
            done = S["ev%d_%d" % (i, h)] if i < NE - 4 else (S.evs if h else S.evv)
            if h == 0:
                V.wait_ge(S["mm%d_0" % i], 1)
                V.tensor_copy(out, T.ps[:, 512 * bank:512 * bank + HALF]).then_inc(done, 1)
            else:
                C.wait_ge(S["mm%d_1" % i], 1)
                C.activation(out, T.ps[:, 512 * bank:512 * bank + HALF], COPY).then_inc(done, 1)

    for q in (V, C):
        q.wait_ge(S.offy, 1)
        for i in range(NE - 4):
            for h in (0, 1):
                q.wait_ge(S["ev%d_%d" % (i, h)], 1)
        q.wait_ge(S.evv, 4)
        q.wait_ge(S.evs, 4)
    V.tensor_copy(T.yb[:, 0:128], T.res[:].indirect(T.offy[:, 0:8])).then_inc(S.yv, 1)
    C.activation(T.yb[:, 128:256], T.res[:].indirect(T.offy[:, 8:16]), COPY).then_inc(S.ys, 1)
    SY.wait_ge(S.yv, 1)
    SY.dma_start(T.y[:, 0:128], T.yb[:, 0:128]).then_inc(S.y0, 16)
    C.wait_ge(S.ys, 1)
    C.dma_start(T.y[:, 128:256], T.yb[:, 128:256]).then_inc(S.y1, 16)
    SY.wait_ge(S.y0, 16)
    C.wait_ge(S.y1, 16)
    g.wait_ge(S.loc, sent[0])
